import numpy as np
import ml_dtypes


def mxq(x, axis, fmt="e4m3"):
    dtype, down = {"e4m3": (ml_dtypes.float8_e4m3fn, 7), "e5m2": (ml_dtypes.float8_e5m2, 14)}[fmt]
    v = np.moveaxis(np.asarray(x, np.float32).astype(ml_dtypes.bfloat16).astype(np.float64), axis, -1)
    blocks = v.reshape(v.shape[:-1] + (-1, 32))
    amax = np.abs(blocks).max(-1, keepdims=True)
    byte = np.maximum(np.where(amax > 0, np.frexp(amax)[1] - 1 + 127, 0) - down, 1)
    scale = np.exp2(byte - 127.0)
    codes = (blocks / scale).astype(np.float32).astype(dtype).astype(np.float64)
    return np.moveaxis((codes * scale).reshape(v.shape), -1, axis)


WIDE = False


def mx_kscale(k):
    if not WIDE:
        return np.ones(k)
    levels = np.array([10, -10, 5, -5, 0])
    if k % 512:
        return np.exp2(np.random.permutation(np.resize(levels, k // 32))).repeat(32)
    a = np.empty((k // 512, 16))
    for p in range(k // 512):
        a[p, :8] = np.random.permutation(np.resize(levels, 8))
        for g in range(8):
            far = levels[np.abs(levels - a[p, g]) >= 10]
            a[p, g + 8] = far[np.random.randint(len(far))]
    return np.exp2(a.ravel()).repeat(32)


def f64(x):
    return np.asarray(x).astype(np.float64)


def striped(idx):
    return np.tile(idx.reshape(-1, 16).T, (8, 1)).astype(np.uint16)


def unstriped(offs):
    return offs[:16].T.reshape(-1).astype(np.int64)


E2M1 = np.array([0.0, 0.5, 1.0, 1.5, 2.0, 3.0, 4.0, 6.0, -0.0, -0.5, -1.0, -1.5, -2.0, -3.0, -4.0, -6.0])


def pack_weight(w, fmt):
    k, n = w.shape
    w = f64(np.asarray(w, np.float32).astype(ml_dtypes.bfloat16)).reshape(k // 32, 32, n)
    amax = np.abs(w).max(1)
    if fmt == "e4m3":
        byte = np.frexp(amax)[1] - 1 + 127 - 7
    else:
        mant, ex = np.frexp(amax / 6.0)
        byte = np.where(mant > 0.5, ex, ex - 1) + 127
    byte = np.clip(np.where(amax > 0, byte, 1), 1, 254)
    scaled = (w * np.exp2(127.0 - byte)[:, None, :]).reshape(k, n).astype(np.float32)
    by_word = np.ascontiguousarray(scaled.reshape(k // 512, 128, 4, n).transpose(0, 1, 3, 2))
    if fmt == "e4m3":
        words = by_word.astype(ml_dtypes.float8_e4m3fn).view(np.uint8)
    else:
        c = by_word.astype(ml_dtypes.float4_e2m1fn).view(np.uint8) & 0xF
        words = (c[..., 0::2] | (c[..., 1::2] << 4)).reshape(k // 512, 128, 2 * n)
    return np.ascontiguousarray(words), np.ascontiguousarray(byte.astype(np.uint8).reshape(k // 512, 16, n))


def unpack_weight(words, scales, fmt):
    g, _, n = scales.shape
    words = np.ascontiguousarray(words).reshape(g, 128, n, -1)
    if fmt == "e4m3":
        vals = words.view(ml_dtypes.float8_e4m3fn).astype(np.float64)
    else:
        nib = np.empty((g, 128, n, 4), np.uint8)
        nib[..., 0::2] = words & 0xF
        nib[..., 1::2] = words >> 4
        vals = E2M1[nib]
    vals = vals * np.repeat(np.exp2(scales.astype(np.float64) - 127.0), 8, axis=1)[..., None]
    return vals.transpose(0, 1, 3, 2).reshape(g * 512, n)


def gelu(v):
    return 0.5 * v * (1.0 + np.tanh(np.sqrt(2.0 / np.pi) * (v + 0.044715 * v**3)))


def striped8(idx):
    return np.concatenate([v.reshape(-1, 16).T for v in idx]).astype(np.uint16)


def unstriped8(offs):
    return np.stack([offs[16 * g:16 * g + 16].T.reshape(-1) for g in range(8)]).astype(np.int64)


def runs(v, idx8):
    k = np.arange(v.shape[0])
    return v[k[:, None], idx8[k % 512 // 64]]


K, K2, H, N, T, S, T2 = 1024, 512, 512, 384, 2048, 1024, 2048

def setup_inputs():
    n = np.random.standard_normal
    s = mx_kscale(K)[:, None]
    s2 = mx_kscale(K2)[:, None]
    u = mx_kscale(H)[:, None]
    tab_words, tab_scales = pack_weight(n((K, T)) * s, "e4m3")
    tab2_words, tab2_scales = pack_weight(n((K2, T)) * s2, "e4m3")
    w2_words, w2_scales = pack_weight(1.1 * n((K2, H)) / np.sqrt(K2) / s2, "e2m1")
    w3_words, w3_scales = pack_weight(0.5 * n((K, H)) / np.sqrt(K) / s, "e4m3")
    w5_words, w5_scales = pack_weight(n((H, N)) / np.sqrt(H) / u, "e2m1")
    return {
        "tab_words": tab_words, "tab_scales": tab_scales,
        "tab2_words": tab2_words, "tab2_scales": tab2_scales,
        "offs": striped8(np.stack([np.random.permutation(T)[:S] for _ in range(8)])),
        "offs2": striped(np.random.permutation(T)[:S]),
        "offs3": striped(np.random.permutation(T2)[:S]),
        "w1": (1.1 * n((K, H)) / np.sqrt(K) / s).astype(np.float32),
        "w2_words": w2_words, "w2_scales": w2_scales,
        "w3_words": w3_words, "w3_scales": w3_scales,
        "w4": (0.5 * n((K2, H)) / np.sqrt(K2) / s2).astype(np.float32),
        "gain": (np.exp(0.4 * n(H)) * u[:, 0]).astype(np.float32),
        "w5_words": w5_words, "w5_scales": w5_scales,
        "by": (0.5 * n(N)).astype(np.float32),
        "page1": n((N, T2)).astype(np.float32),
        "wgo": np.exp(0.3 * n((128, S))).astype(np.float32)}

def reference(tab_words, tab_scales, tab2_words, tab2_scales, offs, offs2, offs3, w1, w2_words, w2_scales,
              w3_words, w3_scales, w4, gain, w5_words, w5_scales, by, page1, wgo):
    v = runs(unpack_weight(tab_words, tab_scales, "e4m3"), unstriped8(offs))
    v2 = unpack_weight(tab2_words, tab2_scales, "e4m3")[:, unstriped(offs2)]
    p = mxq(f64(w1), 0, "e4m3").T @ v + unpack_weight(w2_words, w2_scales, "e2m1").T @ v2
    q = unpack_weight(w3_words, w3_scales, "e4m3").T @ v + mxq(f64(w4), 0, "e4m3").T @ v2
    h = f64(gain)[:, None] * np.maximum(np.tanh(p), np.abs(q))
    y = (unpack_weight(w5_words, w5_scales, "e2m1").T @ mxq(h, 0, "e4m3")) + f64(by)[:, None]
    out = f64(page1).copy()
    out[:, unstriped(offs3)] = np.tile(f64(wgo), (N // 128, 1)) * y
    return out

@@ -1,0 +1,272 @@
+from contextlib import ExitStack
+
+import concourse.mybir as mybir
+
+K, K2, H, N, T, S, T2 = 1024, 512, 512, 384, 2048, 1024, 2048
+FLOPS = 2 * S * (2 * (K + K2) * H + H * N)
+
+F32 = mybir.dt.float32
+BF16 = mybir.dt.bfloat16
+I32 = mybir.dt.int32
+U32 = mybir.dt.uint32
+U16 = mybir.dt.uint16
+U8 = mybir.dt.uint8
+FP8X4 = mybir.dt.float8_e4m3fn_x4
+FP4X4 = mybir.dt.float4_e2m1fn_x4
+ACT = mybir.ActivationFunctionType
+ALU = mybir.AluOpType
+
+P = 128
+PACK = 4
+K_PASS = P * PACK
+CHUNK = 256
+CHUNKS = S // CHUNK
+LIST_COLS = CHUNK // 16
+ROW_TILES = N // P
+BUFS = {"y0": 2, "y1": 2, "late": 1}
+
+
+def tile_list_stem_transition_scores_kernel(
+    tc, tab_words, tab_scales, tab2_words, tab2_scales, offs, offs2, offs3, w1, w2_words, w2_scales,
+    w3_words, w3_scales, w4, gain, w5_words, w5_scales, by, page1, wgo, out,
+):
+    nc = tc.nc
+    with ExitStack() as ctx:
+        keep = ctx.enter_context(tc.tile_pool(name="keep", bufs=1))
+        ring = ctx.enter_context(tc.tile_pool(name="ring", bufs=2))
+        psum = ctx.enter_context(tc.psum_pool(name="psum", bufs=1))
+
+        def kept(name, shape, dtype):
+            return keep.tile(shape, dtype, name=name, align_bytes=64)
+
+        def load_words(name, words):
+            tile = kept(name, [P, words.shape[1]], U32)
+            nc.sync.dma_start(tile[:].bitcast(I32), words.rearrange("p t i -> p (t i)").bitcast(I32))
+            return tile
+
+        def load_rows(name, rows):
+            tile = kept(name, [P, PACK, rows.shape[1]], F32)
+            nc.sync.dma_start(tile[:], rows.rearrange("(p j) c -> p j c", j=PACK))
+            return tile
+
+        def zeroed_bytes(name, width):
+            tile = kept(name, [P, width], U8)
+            nc.vector.memset(tile[:].bitcast(I32), 0)
+            return tile
+
+        def load_scale_rows(queue, tile, first, scales, quadrants):
+            passes = scales.shape[0]
+            for d in quadrants:
+                rows = slice(32 * d + first, 32 * d + first + 4 * passes)
+                queue.dma_start(tile[rows, :].bitcast(I32), scales[:, 4 * d : 4 * d + 4, :].bitcast(I32))
+
+        def quantise_weight(name, parts):
+            grouped = kept(name + "_bf16", [P, PACK, P, PACK], BF16)
+            share = P // len(parts)
+            for u, raw in enumerate(parts):
+                nc.scalar.copy(
+                    grouped[:, :, u * share : (u + 1) * share, :].rearrange("p t m j -> p m j t"),
+                    raw[:].rearrange("p j (m t) -> p m j t", t=PACK),
+                )
+            codes = kept(name + "_codes", [P, H], U32)
+            plane = kept(name + "_plane", [P, H], U8)
+            nc.vector.quantize_mx(
+                out=codes[:].bitcast(FP8X4), scales=plane[:], in_=grouped[:].rearrange("p t m j -> p (t m j)")
+            )
+            return codes, plane
+
+        def deal_columns(name, raw, dtype):
+            dealt = kept(name, [P, H], dtype)
+            view = I32 if dtype == U32 else dtype
+            nc.vector.tensor_copy(
+                dealt[:].bitcast(view).rearrange("p (t m) -> p m t", t=PACK),
+                raw.bitcast(view).rearrange("p (m t) -> p m t", t=PACK),
+            )
+            return dealt
+
+        def gather(picked, window, offsets):
+            nc.vector.tensor_copy(picked, window[:].indirect(offsets))
+
+        tab_bytes = kept("tab_bytes", [P, T], U8)
+        nc.vector.memset(tab_bytes[:, 0 : T // 2].bitcast(I32), 0)
+        nc.gpsimd.memset(tab_bytes[:, T // 2 : T].bitcast(I32), 0)
+        tab2_bytes = zeroed_bytes("tab2_bytes", T)
+        w23_bytes = zeroed_bytes("w23_bytes", H)
+        w5_plane = zeroed_bytes("w5_plane", N)
+
+        lists = keep.tile([P, S // 16], U16, name="lists")
+        nc.sync.dma_start(lists[:], offs)
+        gain_sb = kept("gain_sb", [P, PACK], F32)
+        nc.sync.dma_start(gain_sb[:], gain.rearrange("(p t) -> p t", t=PACK))
+        list2 = keep.tile([P, S // 16], U16, name="list2")
+        nc.sync.dma_start(list2[:], offs2)
+        list3 = keep.tile([P, S // 16], U16, name="list3")
+        nc.sync.dma_start(list3[:], offs3)
+        by_parity = tab_scales.rearrange("a (g r) t -> r g a t", r=2)
+        for r in range(2):
+            nc.sync.dma_start(tab_bytes[r:P:8, :].bitcast(I32), by_parity[r].bitcast(I32))
+        tab_pass0 = load_words("tab_pass0", tab_words[0])
+        load_scale_rows(nc.gpsimd, w23_bytes, 4, w3_scales, range(4))
+        w1_raw0 = load_rows("w1_raw0", w1[0:K_PASS, :])
+        load_scale_rows(nc.sync, tab2_bytes, 0, tab2_scales, range(4))
+        tab_pass1 = load_words("tab_pass1", tab_words[1])
+        w1_raw1 = load_rows("w1_raw1", w1[K_PASS:K, :])
+
+        picked_bytes = kept("picked_bytes", [P, S], U8)
+        gather(picked_bytes[:], tab_bytes, lists[:])
+        v_planes = kept("v_planes", [P, S], U8)
+        nc.vector.tensor_copy(v_planes[:].bitcast(I32), picked_bytes[:].bitcast(I32))
+        for a in range(2):
+            for r in range(2):
+                nc.sync.dma_start(
+                    v_planes[8 * a + 2 + r : P : 32, :].bitcast(I32),
+                    picked_bytes[16 + 8 * a + r : P : 32, :].bitcast(I32),
+                )
+
+        tab2_pass = load_words("tab2_pass", tab2_words[0])
+        load_scale_rows(nc.sync, w23_bytes, 0, w2_scales, range(4))
+        w4_raw = [load_rows("w4_raw%d" % u, w4[:, u * H // 2 : (u + 1) * H // 2]) for u in range(2)]
+        w2_raw = kept("w2_raw", [P, 2 * H], U8)
+        nc.sync.dma_start(w2_raw[:].bitcast(I32), w2_words[0].bitcast(I32))
+        w3_raw = [load_words("w3_raw%d" % a, w3_words[a]) for a in range(2)]
+        w5_sb = kept("w5_sb", [P, 2 * N], U8)
+        nc.sync.dma_start(w5_sb[:].bitcast(I32), w5_words[0].bitcast(I32))
+        wgo_sb = kept("wgo_sb", [P, S], F32)
+        nc.sync.dma_start(wgo_sb[:], wgo)
+        by_sb = kept("by_sb", [P, ROW_TILES], F32)
+        with nc.allow_non_contiguous_dma(reason="one bias value for each partition and row tile"):
+            nc.sync.dma_start(by_sb[:], by.rearrange("(n p) -> p n", p=P))
+        pages = [kept("page%d" % n, [P, T2], F32) for n in range(ROW_TILES)]
+        nc.sync.dma_start(pages[0][:], page1[0:P, :])
+        load_scale_rows(nc.sync, w5_plane, 0, w5_scales, range(4))
+        for n in range(1, ROW_TILES):
+            nc.sync.dma_start(pages[n][:], page1[n * P : (n + 1) * P, :])
+
+        def list_slice(tile, first_chunk, chunks):
+            return tile[:, first_chunk * LIST_COLS : (first_chunk + chunks) * LIST_COLS]
+
+        def gather_chunks(name, window, offsets):
+            chunks = []
+            for c in range(CHUNKS):
+                picked = kept("%s_chunk%d" % (name, c), [P, CHUNK], U32)
+                gather(picked[:], window, list_slice(offsets, c, 1))
+                chunks.append(picked)
+            return chunks
+
+        v0_chunks = gather_chunks("v0", tab_pass0, lists)
+        v2_plane = kept("v2_plane", [P, S], U8)
+        gather(v2_plane[:], tab2_bytes, list2[:])
+        w1_q0 = quantise_weight("w1_pass0", [w1_raw0])
+        v1_chunks = gather_chunks("v1", tab_pass1, lists)
+        w1_q1 = quantise_weight("w1_pass1", [w1_raw1])
+        w23_planes = deal_columns("w23_planes", w23_bytes[:], U8)
+        v2_chunks = gather_chunks("v2", tab2_pass, list2)
+        w2_codes = deal_columns("w2_codes", w2_raw[:].bitcast(U16), U16)
+        w3_codes = [deal_columns("w3_codes%d" % a, w3_raw[a][:], U32) for a in range(2)]
+        w4_q = quantise_weight("w4", w4_raw)
+
+
+        def fp8_weight(codes, plane, first):
+            return lambda t: (codes[:, t * P : (t + 1) * P].bitcast(FP8X4), plane[first:P, t * P : (t + 1) * P])
+
+        def fp4_weight(codes, plane):
+            return lambda t: (codes[:, t * P : (t + 1) * P].bitcast(FP4X4), plane[:, t * P : (t + 1) * P])
+
+        w1_pass = [fp8_weight(*w1_q0, 0), fp8_weight(*w1_q1, 0)]
+        w2_pass = fp4_weight(w2_codes[:], w23_planes)
+        w3_pass = [fp8_weight(w3_codes[a], w23_planes, 4 + 4 * a) for a in range(2)]
+        w4_pass = fp8_weight(*w4_q, 0)
+        w5_pass = fp4_weight(w5_sb[:].bitcast(U16), w5_plane)
+
+        def sum_pair(terms, pair):
+            bank = psum.tile([P, 2, CHUNK], F32, name="pq", tag="pq", bufs=6)
+            steps = [(weight, moving, u) for weight, moving in terms for u in range(2)]
+            for i, (weight, moving, u) in enumerate(steps):
+                codes, plane = weight(2 * pair + u)
+                nc.tensor.matmul_mx(
+                    out=bank[:, u, :], lhsT=codes, lhsT_scale=plane, rhs=moving[0], rhs_scale=moving[1],
+                    start=(i == 0), stop=(i == len(steps) - 1),
+                )
+            return bank
+
+        def put(n, y_bank, first_chunk, chunks, tag):
+            width = chunks * CHUNK
+            y = ring.tile([P, width], F32, name="y", tag=tag, bufs=BUFS[tag], align_bytes=64)
+            nc.scalar.activation(y[:], y_bank, ACT.Identity, bias=by_sb[:, n : n + 1])
+            cols = slice(first_chunk * CHUNK, first_chunk * CHUNK + width)
+            nc.vector.tensor_tensor(
+                pages[n][:].indirect(list_slice(list3, first_chunk, chunks)), y[:], wgo_sb[:, cols], ALU.mult
+            )
+            return y
+
+        def y_product(target, n, h):
+            codes, plane = w5_pass(n)
+            nc.tensor.matmul_mx(
+                out=target, lhsT=codes, lhsT_scale=plane, rhs=h[0][:].bitcast(FP8X4), rhs_scale=h[1][:],
+                start=True, stop=True,
+            )
+
+        def first_stage(c):
+            cols = slice(c * CHUNK, (c + 1) * CHUNK)
+            v_moving = [
+                (v0_chunks[c][:].bitcast(FP8X4), v_planes[0:P, cols]),
+                (v1_chunks[c][:].bitcast(FP8X4), v_planes[8:P, cols]),
+            ]
+            v2_moving = (v2_chunks[c][:].bitcast(FP8X4), v2_plane[:, cols])
+            p_terms = [(w1_pass[0], v_moving[0]), (w1_pass[1], v_moving[1]), (w2_pass, v2_moving)]
+            q_terms = [(w3_pass[0], v_moving[0]), (w3_pass[1], v_moving[1]), (w4_pass, v2_moving)]
+            fits = []
+            for pair in range(2):
+                fit = ring.tile([P, 2, CHUNK], F32, name="fit", bufs=4)
+                nc.scalar.activation(fit[:], sum_pair(p_terms, pair)[:], ACT.Tanh)
+                fits.append(fit)
+            stronger = ring.tile([P, PACK, CHUNK], F32, name="stronger")
+            for pair in range(2):
+                contrast = ring.tile([P, 2, CHUNK], F32, name="contrast", bufs=4)
+                nc.scalar.activation(contrast[:], sum_pair(q_terms, pair)[:], ACT.Abs)
+                nc.vector.tensor_tensor(stronger[:, 2 * pair : 2 * pair + 2, :], fits[pair][:], contrast[:], ALU.max)
+            return stronger
+
+        def quantise_h(stronger, on_vector):
+            h_grouped = ring.tile([P, CHUNK, PACK], BF16, name="h_grouped", align_bytes=64)
+            walk = h_grouped[:].rearrange("p (c i) t -> p c t i", i=4)
+            if on_vector:
+                gains = gain_sb[:].rearrange("p (c t i) -> p c t i", c=1, i=1).to_broadcast([P, CHUNK // 4, PACK, 4])
+                nc.vector.tensor_tensor(walk, stronger[:].rearrange("p t (c i) -> p c t i", i=4), gains, ALU.mult)
+            else:
+                h_rows = ring.tile([P, PACK, CHUNK], BF16, name="h_rows", tag="late", bufs=BUFS["late"], align_bytes=64)
+                for t in range(PACK):
+                    nc.scalar.activation(h_rows[:, t, :], stronger[:, t, :], ACT.Copy, scale=gain_sb[:, t : t + 1])
+                nc.scalar.copy(walk, h_rows[:].rearrange("p t (c i) -> p c t i", i=4))
+            h_codes = ring.tile([P, CHUNK], U32, name="h_codes", bufs=CHUNKS, align_bytes=64)
+            h_plane = ring.tile([P, CHUNK], U8, name="h_plane", bufs=CHUNKS, align_bytes=64)
+            nc.vector.quantize_mx(
+                out=h_codes[:].bitcast(FP8X4), scales=h_plane[:], in_=h_grouped[:].rearrange("p c t -> p (c t)")
+            )
+            return h_codes, h_plane
+
+        def second_stage(c):
+            y_bank = psum.tile([P, 2, CHUNK], F32, name="y_bank")
+            for n in range(2):
+                y_product(y_bank[:, n, :], n, h_chunks[c])
+            return [put(n, y_bank[:, n, :], c, 1, "y%d" % n) for n in range(2)]
+
+        def last_row_tile(first_chunk, chunks):
+            y_last = psum.tile([P, chunks, CHUNK], F32, name="y_last")
+            for u in range(chunks):
+                y_product(y_last[:, u, :], 2, h_chunks[first_chunk + u])
+            put(2, y_last[:].rearrange("p u c -> p (u c)"), first_chunk, chunks, "late")
+
+        h_chunks = [quantise_h(first_stage(0), True)]
+        for c in range(CHUNKS):
+            if c + 1 < CHUNKS:
+                pairs = first_stage(c + 1)
+            ys = second_stage(c)
+            if c + 1 < CHUNKS:
+                h_chunks.append(quantise_h(pairs, False))
+                if c >= 1:
+                    last_row_tile(c - 1, 1)
+        last_row_tile(CHUNKS - 2, 2)
+
+        for n in range(ROW_TILES):
+            nc.sync.dma_start(out[n * P : (n + 1) * P, :], pages[n][:])

@@ -36,8 +36,8 @@ def tile_list_stem_transition_scores_kernel(
         ring = ctx.enter_context(tc.tile_pool(name="ring", bufs=2))
         psum = ctx.enter_context(tc.psum_pool(name="psum", bufs=1))
 
-        def kept(name, shape, dtype):
-            return keep.tile(shape, dtype, name=name, align_bytes=64)
+        def kept(name, shape, dtype, tag=None):
+            return keep.tile(shape, dtype, name=name, tag=tag or name, align_bytes=64)
 
         def load_words(name, words):
             tile = kept(name, [P, words.shape[1]], U32)
@@ -75,42 +75,38 @@ def tile_list_stem_transition_scores_kernel(
             )
             return codes, plane
 
-        def deal_columns(name, raw, dtype):
-            dealt = kept(name, [P, H], dtype)
-            view = I32 if dtype == U32 else dtype
+        def deal_columns(dealt, raw):
             nc.vector.tensor_copy(
-                dealt[:].bitcast(view).rearrange("p (t m) -> p m t", t=PACK),
-                raw.bitcast(view).rearrange("p (m t) -> p m t", t=PACK),
+                dealt.rearrange("p (t m) -> p m t", t=PACK), raw.rearrange("p (m t) -> p m t", t=PACK)
             )
-            return dealt
 
         def gather(picked, window, offsets):
             nc.vector.tensor_copy(picked, window[:].indirect(offsets))
 
-        tab_bytes = kept("tab_bytes", [P, T], U8)
-        nc.vector.memset(tab_bytes[:, 0 : T // 2].bitcast(I32), 0)
-        nc.gpsimd.memset(tab_bytes[:, T // 2 : T].bitcast(I32), 0)
-        tab2_bytes = zeroed_bytes("tab2_bytes", T)
         w23_bytes = zeroed_bytes("w23_bytes", H)
+        tab_bytes = zeroed_bytes("tab_bytes", T)
+        tab2_bytes = zeroed_bytes("tab2_bytes", T)
         w5_plane = zeroed_bytes("w5_plane", N)
 
         lists = keep.tile([P, S // 16], U16, name="lists")
         nc.sync.dma_start(lists[:], offs)
-        gain_sb = kept("gain_sb", [P, PACK], F32)
-        nc.sync.dma_start(gain_sb[:], gain.rearrange("(p t) -> p t", t=PACK))
         list2 = keep.tile([P, S // 16], U16, name="list2")
         nc.sync.dma_start(list2[:], offs2)
-        list3 = keep.tile([P, S // 16], U16, name="list3")
-        nc.sync.dma_start(list3[:], offs3)
+        load_scale_rows(nc.sync, w23_bytes, 0, w2_scales, range(3))
+        load_scale_rows(nc.gpsimd, w23_bytes, 4, w3_scales, range(4))
         by_parity = tab_scales.rearrange("a (g r) t -> r g a t", r=2)
         for r in range(2):
             nc.sync.dma_start(tab_bytes[r:P:8, :].bitcast(I32), by_parity[r].bitcast(I32))
         tab_pass0 = load_words("tab_pass0", tab_words[0])
-        load_scale_rows(nc.gpsimd, w23_bytes, 4, w3_scales, range(4))
         w1_raw0 = load_rows("w1_raw0", w1[0:K_PASS, :])
-        load_scale_rows(nc.sync, tab2_bytes, 0, tab2_scales, range(4))
-        tab_pass1 = load_words("tab_pass1", tab_words[1])
+        by_row = tab2_scales[0].rearrange("(d r) t -> r d t", r=4)
+        for r in range(4):
+            nc.sync.dma_start(tab2_bytes[r:P:32, :].bitcast(I32), by_row[r].bitcast(I32))
+        w2_raw = kept("w2_raw", [P, 2 * H], U8)
+        nc.sync.dma_start(w2_raw[:].bitcast(I32), w2_words[0].bitcast(I32))
         w1_raw1 = load_rows("w1_raw1", w1[K_PASS:K, :])
+        tab_pass1 = load_words("tab_pass1", tab_words[1])
+        load_scale_rows(nc.sync, w23_bytes, 0, w2_scales, range(3, 4))
 
         picked_bytes = kept("picked_bytes", [P, S], U8)
         gather(picked_bytes[:], tab_bytes, lists[:])
@@ -124,15 +120,16 @@ def tile_list_stem_transition_scores_kernel(
                 )
 
         tab2_pass = load_words("tab2_pass", tab2_words[0])
-        load_scale_rows(nc.sync, w23_bytes, 0, w2_scales, range(4))
         w4_raw = [load_rows("w4_raw%d" % u, w4[:, u * H // 2 : (u + 1) * H // 2]) for u in range(2)]
-        w2_raw = kept("w2_raw", [P, 2 * H], U8)
-        nc.sync.dma_start(w2_raw[:].bitcast(I32), w2_words[0].bitcast(I32))
         w3_raw = [load_words("w3_raw%d" % a, w3_words[a]) for a in range(2)]
+        gain_sb = kept("gain_sb", [P, PACK], F32)
+        nc.sync.dma_start(gain_sb[:], gain.rearrange("(p t) -> p t", t=PACK))
         w5_sb = kept("w5_sb", [P, 2 * N], U8)
         nc.sync.dma_start(w5_sb[:].bitcast(I32), w5_words[0].bitcast(I32))
         wgo_sb = kept("wgo_sb", [P, S], F32)
         nc.sync.dma_start(wgo_sb[:], wgo)
+        list3 = keep.tile([P, S // 16], U16, name="list3")
+        nc.sync.dma_start(list3[:], offs3)
         by_sb = kept("by_sb", [P, ROW_TILES], F32)
         with nc.allow_non_contiguous_dma(reason="one bias value for each partition and row tile"):
             nc.sync.dma_start(by_sb[:], by.rearrange("(n p) -> p n", p=P))
@@ -145,24 +142,28 @@ def tile_list_stem_transition_scores_kernel(
         def list_slice(tile, first_chunk, chunks):
             return tile[:, first_chunk * LIST_COLS : (first_chunk + chunks) * LIST_COLS]
 
-        def gather_chunks(name, window, offsets):
+        def gather_chunks(name, window, offsets, runs):
             chunks = []
-            for c in range(CHUNKS):
-                picked = kept("%s_chunk%d" % (name, c), [P, CHUNK], U32)
-                gather(picked[:], window, list_slice(offsets, c, 1))
-                chunks.append(picked)
+            for run in runs:
+                picked = kept("%s_from%d" % (name, len(chunks)), [P, run, CHUNK], U32)
+                gather(picked[:].rearrange("p u c -> p (u c)"), window, list_slice(offsets, len(chunks), run))
+                chunks.extend(picked[:, u, :] for u in range(run))
             return chunks
 
-        v0_chunks = gather_chunks("v0", tab_pass0, lists)
+        v0_chunks = gather_chunks("v0", tab_pass0, lists, [4])
         v2_plane = kept("v2_plane", [P, S], U8)
         gather(v2_plane[:], tab2_bytes, list2[:])
         w1_q0 = quantise_weight("w1_pass0", [w1_raw0])
-        v1_chunks = gather_chunks("v1", tab_pass1, lists)
+        w2_codes = kept("w2_codes", [P, H], U16)
+        deal_columns(w2_codes[:], w2_raw[:].bitcast(U16))
         w1_q1 = quantise_weight("w1_pass1", [w1_raw1])
-        w23_planes = deal_columns("w23_planes", w23_bytes[:], U8)
-        v2_chunks = gather_chunks("v2", tab2_pass, list2)
-        w2_codes = deal_columns("w2_codes", w2_raw[:].bitcast(U16), U16)
-        w3_codes = [deal_columns("w3_codes%d" % a, w3_raw[a][:], U32) for a in range(2)]
+        w23_planes = kept("w23_planes", [P, H], U8)
+        deal_columns(w23_planes[:], w23_bytes[:])
+        v1_chunks = gather_chunks("v1", tab_pass1, lists, [2, 2])
+        v2_chunks = gather_chunks("v2", tab2_pass, list2, [1, 1, 2])
+        w3_codes = [kept("w3_codes%d" % a, [P, H], U32) for a in range(2)]
+        for a in range(2):
+            deal_columns(w3_codes[a][:].bitcast(I32), w3_raw[a][:].bitcast(I32))
         w4_q = quantise_weight("w4", w4_raw)
 
 
@@ -209,20 +210,20 @@ def tile_list_stem_transition_scores_kernel(
         def first_stage(c):
             cols = slice(c * CHUNK, (c + 1) * CHUNK)
             v_moving = [
-                (v0_chunks[c][:].bitcast(FP8X4), v_planes[0:P, cols]),
-                (v1_chunks[c][:].bitcast(FP8X4), v_planes[8:P, cols]),
+                (v0_chunks[c].bitcast(FP8X4), v_planes[0:P, cols]),
+                (v1_chunks[c].bitcast(FP8X4), v_planes[8:P, cols]),
             ]
-            v2_moving = (v2_chunks[c][:].bitcast(FP8X4), v2_plane[:, cols])
+            v2_moving = (v2_chunks[c].bitcast(FP8X4), v2_plane[:, cols])
             p_terms = [(w1_pass[0], v_moving[0]), (w1_pass[1], v_moving[1]), (w2_pass, v2_moving)]
             q_terms = [(w3_pass[0], v_moving[0]), (w3_pass[1], v_moving[1]), (w4_pass, v2_moving)]
             fits = []
             for pair in range(2):
-                fit = ring.tile([P, 2, CHUNK], F32, name="fit", bufs=4)
+                fit = kept("fit", [P, 2, CHUNK], F32, "w4_raw%d" % (1 - pair))
                 nc.scalar.activation(fit[:], sum_pair(p_terms, pair)[:], ACT.Tanh)
                 fits.append(fit)
             stronger = ring.tile([P, PACK, CHUNK], F32, name="stronger")
             for pair in range(2):
-                contrast = ring.tile([P, 2, CHUNK], F32, name="contrast", bufs=4)
+                contrast = ring.tile([P, 2, CHUNK], F32, name="contrast")
                 nc.scalar.activation(contrast[:], sum_pair(q_terms, pair)[:], ACT.Abs)
                 nc.vector.tensor_tensor(stronger[:, 2 * pair : 2 * pair + 2, :], fits[pair][:], contrast[:], ALU.max)
             return stronger
@@ -261,11 +262,12 @@ def tile_list_stem_transition_scores_kernel(
         for c in range(CHUNKS):
             if c + 1 < CHUNKS:
                 pairs = first_stage(c + 1)
-            ys = second_stage(c)
-            if c + 1 < CHUNKS:
+            if c == 0:
+                h_chunks.append(quantise_h(pairs, True))
+            second_stage(c)
+            if 1 <= c < CHUNKS - 1:
                 h_chunks.append(quantise_h(pairs, False))
-                if c >= 1:
-                    last_row_tile(c - 1, 1)
+                last_row_tile(c - 1, 1)
         last_row_tile(CHUNKS - 2, 2)
 
         for n in range(ROW_TILES):

@@ -63,8 +63,8 @@ def tile_list_stem_transition_scores_kernel(
         def quantise_weight(name, parts):
             grouped = kept(name + "_bf16", [P, PACK, P, PACK], BF16)
             share = P // len(parts)
-            for u, raw in enumerate(parts):
-                nc.scalar.copy(
+            for u, (raw, cast) in enumerate(parts):
+                cast(
                     grouped[:, :, u * share : (u + 1) * share, :].rearrange("p t m j -> p m j t"),
                     raw[:].rearrange("p j (m t) -> p m j t", t=PACK),
                 )
@@ -83,16 +83,18 @@ def tile_list_stem_transition_scores_kernel(
         def gather(picked, window, offsets):
             nc.vector.tensor_copy(picked, window[:].indirect(offsets))
 
-        w23_bytes = zeroed_bytes("w23_bytes", H)
         tab_bytes = zeroed_bytes("tab_bytes", T)
+        w23_bytes = zeroed_bytes("w23_bytes", H)
         tab2_bytes = zeroed_bytes("tab2_bytes", T)
         w5_plane = zeroed_bytes("w5_plane", N)
 
         lists = keep.tile([P, S // 16], U16, name="lists")
         nc.sync.dma_start(lists[:], offs)
+        w3_raw0 = load_words("w3_raw0", w3_words[0])
+        w2_raw = kept("w2_raw", [P, 2 * H], U8)
+        nc.sync.dma_start(w2_raw[:].bitcast(I32), w2_words[0].bitcast(I32))
         list2 = keep.tile([P, S // 16], U16, name="list2")
         nc.sync.dma_start(list2[:], offs2)
-        load_scale_rows(nc.sync, w23_bytes, 0, w2_scales, range(3))
         load_scale_rows(nc.gpsimd, w23_bytes, 4, w3_scales, range(4))
         by_parity = tab_scales.rearrange("a (g r) t -> r g a t", r=2)
         for r in range(2):
@@ -102,11 +104,15 @@ def tile_list_stem_transition_scores_kernel(
         by_row = tab2_scales[0].rearrange("(d r) t -> r d t", r=4)
         for r in range(4):
             nc.sync.dma_start(tab2_bytes[r:P:32, :].bitcast(I32), by_row[r].bitcast(I32))
-        w2_raw = kept("w2_raw", [P, 2 * H], U8)
-        nc.sync.dma_start(w2_raw[:].bitcast(I32), w2_words[0].bitcast(I32))
+        load_scale_rows(nc.sync, w23_bytes, 0, w2_scales, range(0, 1))
         w1_raw1 = load_rows("w1_raw1", w1[K_PASS:K, :])
         tab_pass1 = load_words("tab_pass1", tab_words[1])
-        load_scale_rows(nc.sync, w23_bytes, 0, w2_scales, range(3, 4))
+        load_scale_rows(nc.sync, w23_bytes, 0, w2_scales, range(1, 2))
+
+        w3_codes = [kept("w3_codes%d" % a, [P, H], U32) for a in range(2)]
+        deal_columns(w3_codes[0][:].bitcast(I32), w3_raw0[:].bitcast(I32))
+        w2_codes = kept("w2_codes", [P, H], U16)
+        deal_columns(w2_codes[:], w2_raw[:].bitcast(U16))
 
         picked_bytes = kept("picked_bytes", [P, S], U8)
         gather(picked_bytes[:], tab_bytes, lists[:])
@@ -120,8 +126,10 @@ def tile_list_stem_transition_scores_kernel(
                 )
 
         tab2_pass = load_words("tab2_pass", tab2_words[0])
-        w4_raw = [load_rows("w4_raw%d" % u, w4[:, u * H // 2 : (u + 1) * H // 2]) for u in range(2)]
-        w3_raw = [load_words("w3_raw%d" % a, w3_words[a]) for a in range(2)]
+        w4_raw0 = load_rows("w4_raw0", w4[:, 0 : H // 2])
+        load_scale_rows(nc.sync, w23_bytes, 0, w2_scales, range(2, 4))
+        w4_raw1 = load_rows("w4_raw1", w4[:, H // 2 : H])
+        w3_raw1 = load_words("w3_raw1", w3_words[1])
         gain_sb = kept("gain_sb", [P, PACK], F32)
         nc.sync.dma_start(gain_sb[:], gain.rearrange("(p t) -> p t", t=PACK))
         w5_sb = kept("w5_sb", [P, 2 * N], U8)
@@ -142,30 +150,27 @@ def tile_list_stem_transition_scores_kernel(
         def list_slice(tile, first_chunk, chunks):
             return tile[:, first_chunk * LIST_COLS : (first_chunk + chunks) * LIST_COLS]
 
-        def gather_chunks(name, window, offsets, runs):
+        def gather_chunks(name, window, offsets, first_chunk, runs, tag=None):
             chunks = []
             for run in runs:
-                picked = kept("%s_from%d" % (name, len(chunks)), [P, run, CHUNK], U32)
-                gather(picked[:].rearrange("p u c -> p (u c)"), window, list_slice(offsets, len(chunks), run))
+                first = first_chunk + len(chunks)
+                picked = kept("%s_from%d" % (name, first), [P, run, CHUNK], U32, tag)
+                gather(picked[:].rearrange("p u c -> p (u c)"), window, list_slice(offsets, first, run))
                 chunks.extend(picked[:, u, :] for u in range(run))
             return chunks
 
-        v0_chunks = gather_chunks("v0", tab_pass0, lists, [4])
+        v0_chunks = gather_chunks("v0", tab_pass0, lists, 0, [4])
         v2_plane = kept("v2_plane", [P, S], U8)
         gather(v2_plane[:], tab2_bytes, list2[:])
-        w1_q0 = quantise_weight("w1_pass0", [w1_raw0])
-        w2_codes = kept("w2_codes", [P, H], U16)
-        deal_columns(w2_codes[:], w2_raw[:].bitcast(U16))
-        w1_q1 = quantise_weight("w1_pass1", [w1_raw1])
+        w1_q0 = quantise_weight("w1_pass0", [(w1_raw0, nc.scalar.copy)])
+        w1_q1 = quantise_weight("w1_pass1", [(w1_raw1, nc.scalar.copy)])
+        v1_chunks = gather_chunks("v1", tab_pass1, lists, 0, [2, 2])
+        v2_chunks = gather_chunks("v2", tab2_pass, list2, 0, [1, 1])
         w23_planes = kept("w23_planes", [P, H], U8)
         deal_columns(w23_planes[:], w23_bytes[:])
-        v1_chunks = gather_chunks("v1", tab_pass1, lists, [2, 2])
-        v2_chunks = gather_chunks("v2", tab2_pass, list2, [1, 1, 2])
-        w3_codes = [kept("w3_codes%d" % a, [P, H], U32) for a in range(2)]
-        for a in range(2):
-            deal_columns(w3_codes[a][:].bitcast(I32), w3_raw[a][:].bitcast(I32))
-        w4_q = quantise_weight("w4", w4_raw)
-
+        deal_columns(w3_codes[1][:].bitcast(I32), w3_raw1[:].bitcast(I32))
+        w4_q = quantise_weight("w4", [(w4_raw0, nc.scalar.copy), (w4_raw1, nc.vector.tensor_copy)])
+        v2_chunks = v2_chunks + gather_chunks("v2", tab2_pass, list2, 2, [2], "w4_bf16")
 
         def fp8_weight(codes, plane, first):
             return lambda t: (codes[:, t * P : (t + 1) * P].bitcast(FP8X4), plane[first:P, t * P : (t + 1) * P])
@@ -218,7 +223,7 @@ def tile_list_stem_transition_scores_kernel(
             q_terms = [(w3_pass[0], v_moving[0]), (w3_pass[1], v_moving[1]), (w4_pass, v2_moving)]
             fits = []
             for pair in range(2):
-                fit = kept("fit", [P, 2, CHUNK], F32, "w4_raw%d" % (1 - pair))
+                fit = ring.tile([P, 2, CHUNK], F32, name="fit", bufs=4)
                 nc.scalar.activation(fit[:], sum_pair(p_terms, pair)[:], ACT.Tanh)
                 fits.append(fit)
             stronger = ring.tile([P, PACK, CHUNK], F32, name="stronger")
@@ -228,17 +233,18 @@ def tile_list_stem_transition_scores_kernel(
                 nc.vector.tensor_tensor(stronger[:, 2 * pair : 2 * pair + 2, :], fits[pair][:], contrast[:], ALU.max)
             return stronger
 
-        def quantise_h(stronger, on_vector):
+        def quantise_h(c, stronger):
             h_grouped = ring.tile([P, CHUNK, PACK], BF16, name="h_grouped", align_bytes=64)
             walk = h_grouped[:].rearrange("p (c i) t -> p c t i", i=4)
-            if on_vector:
+            if c == 0:
                 gains = gain_sb[:].rearrange("p (c t i) -> p c t i", c=1, i=1).to_broadcast([P, CHUNK // 4, PACK, 4])
                 nc.vector.tensor_tensor(walk, stronger[:].rearrange("p t (c i) -> p c t i", i=4), gains, ALU.mult)
             else:
                 h_rows = ring.tile([P, PACK, CHUNK], BF16, name="h_rows", tag="late", bufs=BUFS["late"], align_bytes=64)
                 for t in range(PACK):
                     nc.scalar.activation(h_rows[:, t, :], stronger[:, t, :], ACT.Copy, scale=gain_sb[:, t : t + 1])
-                nc.scalar.copy(walk, h_rows[:].rearrange("p t (c i) -> p c t i", i=4))
+                interleave = nc.vector.tensor_copy if c == 1 else nc.scalar.copy
+                interleave(walk, h_rows[:].rearrange("p t (c i) -> p c t i", i=4))
             h_codes = ring.tile([P, CHUNK], U32, name="h_codes", bufs=CHUNKS, align_bytes=64)
             h_plane = ring.tile([P, CHUNK], U8, name="h_plane", bufs=CHUNKS, align_bytes=64)
             nc.vector.quantize_mx(
@@ -258,16 +264,15 @@ def tile_list_stem_transition_scores_kernel(
                 y_product(y_last[:, u, :], 2, h_chunks[first_chunk + u])
             put(2, y_last[:].rearrange("p u c -> p (u c)"), first_chunk, chunks, "late")
 
-        h_chunks = [quantise_h(first_stage(0), True)]
+        h_chunks = [quantise_h(0, first_stage(0))]
         for c in range(CHUNKS):
             if c + 1 < CHUNKS:
-                pairs = first_stage(c + 1)
-            if c == 0:
-                h_chunks.append(quantise_h(pairs, True))
+                stronger = first_stage(c + 1)
             second_stage(c)
-            if 1 <= c < CHUNKS - 1:
-                h_chunks.append(quantise_h(pairs, False))
-                last_row_tile(c - 1, 1)
+            if c + 1 < CHUNKS:
+                h_chunks.append(quantise_h(c + 1, stronger))
+                if c >= 1:
+                    last_row_tile(c - 1, 1)
         last_row_tile(CHUNKS - 2, 2)
 
         for n in range(ROW_TILES):

from contextlib import ExitStack

import concourse.mybir as mybir

K, K2, H, N, T, S, T2 = 1024, 512, 512, 384, 2048, 1024, 2048
FLOPS = 2 * S * (2 * (K + K2) * H + H * N)

F32 = mybir.dt.float32
BF16 = mybir.dt.bfloat16
I32 = mybir.dt.int32
U32 = mybir.dt.uint32
U16 = mybir.dt.uint16
U8 = mybir.dt.uint8
FP8X4 = mybir.dt.float8_e4m3fn_x4
FP4X4 = mybir.dt.float4_e2m1fn_x4
ACT = mybir.ActivationFunctionType
ALU = mybir.AluOpType

P = 128
PACK = 4
K_PASS = P * PACK
CHUNK = 256
CHUNKS = S // CHUNK
LIST_COLS = CHUNK // 16
ROW_TILES = N // P
BUFS = {"y0": 2, "y1": 2, "late": 1}


def tile_list_stem_transition_scores_kernel(
    tc, tab_words, tab_scales, tab2_words, tab2_scales, offs, offs2, offs3, w1, w2_words, w2_scales,
    w3_words, w3_scales, w4, gain, w5_words, w5_scales, by, page1, wgo, out,
):
    nc = tc.nc
    with ExitStack() as ctx:
        keep = ctx.enter_context(tc.tile_pool(name="keep", bufs=1))
        ring = ctx.enter_context(tc.tile_pool(name="ring", bufs=2))
        psum = ctx.enter_context(tc.psum_pool(name="psum", bufs=1))

        def kept(name, shape, dtype, tag=None):
            return keep.tile(shape, dtype, name=name, tag=tag or name, align_bytes=64)

        def load_words(name, words):
            tile = kept(name, [P, words.shape[1]], U32)
            nc.sync.dma_start(tile[:].bitcast(I32), words.rearrange("p t i -> p (t i)").bitcast(I32))
            return tile

        def load_rows(name, rows):
            tile = kept(name, [P, PACK, rows.shape[1]], F32)
            nc.sync.dma_start(tile[:], rows.rearrange("(p j) c -> p j c", j=PACK))
            return tile

        def zeroed_bytes(name, width):
            tile = kept(name, [P, width], U8)
            nc.vector.memset(tile[:].bitcast(I32), 0)
            return tile

        def load_scale_rows(queue, tile, first, scales, quadrants):
            passes = scales.shape[0]
            for d in quadrants:
                rows = slice(32 * d + first, 32 * d + first + 4 * passes)
                queue.dma_start(tile[rows, :].bitcast(I32), scales[:, 4 * d : 4 * d + 4, :].bitcast(I32))

        def quantise_weight(name, parts):
            grouped = kept(name + "_bf16", [P, PACK, P, PACK], BF16)
            share = P // len(parts)
            for u, (raw, cast) in enumerate(parts):
                cast(
                    grouped[:, :, u * share : (u + 1) * share, :].rearrange("p t m j -> p m j t"),
                    raw[:].rearrange("p j (m t) -> p m j t", t=PACK),
                )
            codes = kept(name + "_codes", [P, H], U32)
            plane = kept(name + "_plane", [P, H], U8)
            nc.vector.quantize_mx(
                out=codes[:].bitcast(FP8X4), scales=plane[:], in_=grouped[:].rearrange("p t m j -> p (t m j)")
            )
            return codes, plane

        def deal_columns(dealt, raw):
            nc.vector.tensor_copy(
                dealt.rearrange("p (t m) -> p m t", t=PACK), raw.rearrange("p (m t) -> p m t", t=PACK)
            )

        def gather(picked, window, offsets):
            nc.vector.tensor_copy(picked, window[:].indirect(offsets))

        tab_bytes = zeroed_bytes("tab_bytes", T)
        w23_bytes = zeroed_bytes("w23_bytes", H)
        tab2_bytes = zeroed_bytes("tab2_bytes", T)
        w5_plane = zeroed_bytes("w5_plane", N)

        lists = keep.tile([P, S // 16], U16, name="lists")
        nc.sync.dma_start(lists[:], offs)
        w3_raw0 = load_words("w3_raw0", w3_words[0])
        w2_raw = kept("w2_raw", [P, 2 * H], U8)
        nc.sync.dma_start(w2_raw[:].bitcast(I32), w2_words[0].bitcast(I32))
        list2 = keep.tile([P, S // 16], U16, name="list2")
        nc.sync.dma_start(list2[:], offs2)
        load_scale_rows(nc.gpsimd, w23_bytes, 4, w3_scales, range(4))
        by_parity = tab_scales.rearrange("a (g r) t -> r g a t", r=2)
        for r in range(2):
            nc.sync.dma_start(tab_bytes[r:P:8, :].bitcast(I32), by_parity[r].bitcast(I32))
        tab_pass0 = load_words("tab_pass0", tab_words[0])
        w1_raw0 = load_rows("w1_raw0", w1[0:K_PASS, :])
        by_row = tab2_scales[0].rearrange("(d r) t -> r d t", r=4)
        for r in range(4):
            nc.sync.dma_start(tab2_bytes[r:P:32, :].bitcast(I32), by_row[r].bitcast(I32))
        load_scale_rows(nc.sync, w23_bytes, 0, w2_scales, range(0, 1))
        w1_raw1 = load_rows("w1_raw1", w1[K_PASS:K, :])
        tab_pass1 = load_words("tab_pass1", tab_words[1])
        load_scale_rows(nc.sync, w23_bytes, 0, w2_scales, range(1, 2))

        w3_codes = [kept("w3_codes%d" % a, [P, H], U32) for a in range(2)]
        deal_columns(w3_codes[0][:].bitcast(I32), w3_raw0[:].bitcast(I32))
        w2_codes = kept("w2_codes", [P, H], U16)
        deal_columns(w2_codes[:], w2_raw[:].bitcast(U16))

        picked_bytes = kept("picked_bytes", [P, S], U8)
        gather(picked_bytes[:], tab_bytes, lists[:])
        v_planes = kept("v_planes", [P, S], U8)
        nc.vector.tensor_copy(v_planes[:].bitcast(I32), picked_bytes[:].bitcast(I32))
        for a in range(2):
            for r in range(2):
                nc.sync.dma_start(
                    v_planes[8 * a + 2 + r : P : 32, :].bitcast(I32),
                    picked_bytes[16 + 8 * a + r : P : 32, :].bitcast(I32),
                )

        tab2_pass = load_words("tab2_pass", tab2_words[0])
        w4_raw0 = load_rows("w4_raw0", w4[:, 0 : H // 2])
        load_scale_rows(nc.sync, w23_bytes, 0, w2_scales, range(2, 4))
        w4_raw1 = load_rows("w4_raw1", w4[:, H // 2 : H])
        w3_raw1 = load_words("w3_raw1", w3_words[1])
        gain_sb = kept("gain_sb", [P, PACK], F32)
        nc.sync.dma_start(gain_sb[:], gain.rearrange("(p t) -> p t", t=PACK))
        w5_sb = kept("w5_sb", [P, 2 * N], U8)
        nc.sync.dma_start(w5_sb[:].bitcast(I32), w5_words[0].bitcast(I32))
        wgo_sb = kept("wgo_sb", [P, S], F32)
        nc.sync.dma_start(wgo_sb[:], wgo)
        list3 = keep.tile([P, S // 16], U16, name="list3")
        nc.sync.dma_start(list3[:], offs3)
        by_sb = kept("by_sb", [P, ROW_TILES], F32)
        with nc.allow_non_contiguous_dma(reason="one bias value for each partition and row tile"):
            nc.sync.dma_start(by_sb[:], by.rearrange("(n p) -> p n", p=P))
        pages = [kept("page%d" % n, [P, T2], F32) for n in range(ROW_TILES)]
        nc.sync.dma_start(pages[0][:], page1[0:P, :])
        load_scale_rows(nc.sync, w5_plane, 0, w5_scales, range(4))
        for n in range(1, ROW_TILES):
            nc.sync.dma_start(pages[n][:], page1[n * P : (n + 1) * P, :])

        def list_slice(tile, first_chunk, chunks):
            return tile[:, first_chunk * LIST_COLS : (first_chunk + chunks) * LIST_COLS]

        def gather_chunks(name, window, offsets, first_chunk, runs, tag=None):
            chunks = []
            for run in runs:
                first = first_chunk + len(chunks)
                picked = kept("%s_from%d" % (name, first), [P, run, CHUNK], U32, tag)
                gather(picked[:].rearrange("p u c -> p (u c)"), window, list_slice(offsets, first, run))
                chunks.extend(picked[:, u, :] for u in range(run))
            return chunks

        v0_chunks = gather_chunks("v0", tab_pass0, lists, 0, [4])
        v2_plane = kept("v2_plane", [P, S], U8)
        gather(v2_plane[:], tab2_bytes, list2[:])
        w1_q0 = quantise_weight("w1_pass0", [(w1_raw0, nc.scalar.copy)])
        w1_q1 = quantise_weight("w1_pass1", [(w1_raw1, nc.scalar.copy)])
        v1_chunks = gather_chunks("v1", tab_pass1, lists, 0, [2, 2])
        v2_chunks = gather_chunks("v2", tab2_pass, list2, 0, [1, 1])
        w23_planes = kept("w23_planes", [P, H], U8)
        deal_columns(w23_planes[:], w23_bytes[:])
        deal_columns(w3_codes[1][:].bitcast(I32), w3_raw1[:].bitcast(I32))
        w4_q = quantise_weight("w4", [(w4_raw0, nc.scalar.copy), (w4_raw1, nc.vector.tensor_copy)])
        v2_chunks = v2_chunks + gather_chunks("v2", tab2_pass, list2, 2, [2], "w4_bf16")

        def fp8_weight(codes, plane, first):
            return lambda t: (codes[:, t * P : (t + 1) * P].bitcast(FP8X4), plane[first:P, t * P : (t + 1) * P])

        def fp4_weight(codes, plane):
            return lambda t: (codes[:, t * P : (t + 1) * P].bitcast(FP4X4), plane[:, t * P : (t + 1) * P])

        w1_pass = [fp8_weight(*w1_q0, 0), fp8_weight(*w1_q1, 0)]
        w2_pass = fp4_weight(w2_codes[:], w23_planes)
        w3_pass = [fp8_weight(w3_codes[a], w23_planes, 4 + 4 * a) for a in range(2)]
        w4_pass = fp8_weight(*w4_q, 0)
        w5_pass = fp4_weight(w5_sb[:].bitcast(U16), w5_plane)

        def sum_pair(terms, pair):
            bank = psum.tile([P, 2, CHUNK], F32, name="pq", tag="pq", bufs=6)
            steps = [(weight, moving, u) for weight, moving in terms for u in range(2)]
            for i, (weight, moving, u) in enumerate(steps):
                codes, plane = weight(2 * pair + u)
                nc.tensor.matmul_mx(
                    out=bank[:, u, :], lhsT=codes, lhsT_scale=plane, rhs=moving[0], rhs_scale=moving[1],
                    start=(i == 0), stop=(i == len(steps) - 1),
                )
            return bank

        def put(n, y_bank, first_chunk, chunks, tag):
            width = chunks * CHUNK
            y = ring.tile([P, width], F32, name="y", tag=tag, bufs=BUFS[tag], align_bytes=64)
            nc.scalar.activation(y[:], y_bank, ACT.Identity, bias=by_sb[:, n : n + 1])
            cols = slice(first_chunk * CHUNK, first_chunk * CHUNK + width)
            nc.vector.tensor_tensor(
                pages[n][:].indirect(list_slice(list3, first_chunk, chunks)), y[:], wgo_sb[:, cols], ALU.mult
            )
            return y

        def y_product(target, n, h):
            codes, plane = w5_pass(n)
            nc.tensor.matmul_mx(
                out=target, lhsT=codes, lhsT_scale=plane, rhs=h[0][:].bitcast(FP8X4), rhs_scale=h[1][:],
                start=True, stop=True,
            )

        def first_stage(c):
            cols = slice(c * CHUNK, (c + 1) * CHUNK)
            v_moving = [
                (v0_chunks[c].bitcast(FP8X4), v_planes[0:P, cols]),
                (v1_chunks[c].bitcast(FP8X4), v_planes[8:P, cols]),
            ]
            v2_moving = (v2_chunks[c].bitcast(FP8X4), v2_plane[:, cols])
            p_terms = [(w1_pass[0], v_moving[0]), (w1_pass[1], v_moving[1]), (w2_pass, v2_moving)]
            q_terms = [(w3_pass[0], v_moving[0]), (w3_pass[1], v_moving[1]), (w4_pass, v2_moving)]
            fits = []
            for pair in range(2):
                fit = ring.tile([P, 2, CHUNK], F32, name="fit", bufs=4)
                nc.scalar.activation(fit[:], sum_pair(p_terms, pair)[:], ACT.Tanh)
                fits.append(fit)
            stronger = ring.tile([P, PACK, CHUNK], F32, name="stronger")
            for pair in range(2):
                contrast = ring.tile([P, 2, CHUNK], F32, name="contrast")
                nc.scalar.activation(contrast[:], sum_pair(q_terms, pair)[:], ACT.Abs)
                nc.vector.tensor_tensor(stronger[:, 2 * pair : 2 * pair + 2, :], fits[pair][:], contrast[:], ALU.max)
            return stronger

        def quantise_h(c, stronger):
            h_grouped = ring.tile([P, CHUNK, PACK], BF16, name="h_grouped", align_bytes=64)
            walk = h_grouped[:].rearrange("p (c i) t -> p c t i", i=4)
            if c == 0:
                gains = gain_sb[:].rearrange("p (c t i) -> p c t i", c=1, i=1).to_broadcast([P, CHUNK // 4, PACK, 4])
                nc.vector.tensor_tensor(walk, stronger[:].rearrange("p t (c i) -> p c t i", i=4), gains, ALU.mult)
            else:
                h_rows = ring.tile([P, PACK, CHUNK], BF16, name="h_rows", tag="late", bufs=BUFS["late"], align_bytes=64)
                for t in range(PACK):
                    nc.scalar.activation(h_rows[:, t, :], stronger[:, t, :], ACT.Copy, scale=gain_sb[:, t : t + 1])
                interleave = nc.vector.tensor_copy if c == 1 else nc.scalar.copy
                interleave(walk, h_rows[:].rearrange("p t (c i) -> p c t i", i=4))
            h_codes = ring.tile([P, CHUNK], U32, name="h_codes", bufs=CHUNKS, align_bytes=64)
            h_plane = ring.tile([P, CHUNK], U8, name="h_plane", bufs=CHUNKS, align_bytes=64)
            nc.vector.quantize_mx(
                out=h_codes[:].bitcast(FP8X4), scales=h_plane[:], in_=h_grouped[:].rearrange("p c t -> p (c t)")
            )
            return h_codes, h_plane

        def second_stage(c):
            y_bank = psum.tile([P, 2, CHUNK], F32, name="y_bank")
            for n in range(2):
                y_product(y_bank[:, n, :], n, h_chunks[c])
            return [put(n, y_bank[:, n, :], c, 1, "y%d" % n) for n in range(2)]

        def last_row_tile(first_chunk, chunks):
            y_last = psum.tile([P, chunks, CHUNK], F32, name="y_last")
            for u in range(chunks):
                y_product(y_last[:, u, :], 2, h_chunks[first_chunk + u])
            put(2, y_last[:].rearrange("p u c -> p (u c)"), first_chunk, chunks, "late")

        h_chunks = [quantise_h(0, first_stage(0))]
        for c in range(CHUNKS):
            if c + 1 < CHUNKS:
                stronger = first_stage(c + 1)
            second_stage(c)
            if c + 1 < CHUNKS:
                h_chunks.append(quantise_h(c + 1, stronger))
                if c >= 1:
                    last_row_tile(c - 1, 1)
        last_row_tile(CHUNKS - 2, 2)

        for n in range(ROW_TILES):
            nc.sync.dma_start(out[n * P : (n + 1) * P, :], pages[n][:])
